import numpy as np
import ml_dtypes


def mxq(x, axis, fmt="e4m3"):
    dtype, down = {"e4m3": (ml_dtypes.float8_e4m3fn, 7), "e5m2": (ml_dtypes.float8_e5m2, 14)}[fmt]
    v = np.moveaxis(np.asarray(x, np.float32).astype(ml_dtypes.bfloat16).astype(np.float64), axis, -1)
    blocks = v.reshape(v.shape[:-1] + (-1, 32))
    amax = np.abs(blocks).max(-1, keepdims=True)
    byte = np.maximum(np.where(amax > 0, np.frexp(amax)[1] - 1 + 127, 0) - down, 1)
    scale = np.exp2(byte - 127.0)
    codes = (blocks / scale).astype(np.float32).astype(dtype).astype(np.float64)
    return np.moveaxis((codes * scale).reshape(v.shape), -1, axis)


WIDE = False


def mx_kscale(k):
    if not WIDE:
        return np.ones(k)
    levels = np.array([10, -10, 5, -5, 0])
    if k % 512:
        return np.exp2(np.random.permutation(np.resize(levels, k // 32))).repeat(32)
    a = np.empty((k // 512, 16))
    for p in range(k // 512):
        a[p, :8] = np.random.permutation(np.resize(levels, 8))
        for g in range(8):
            far = levels[np.abs(levels - a[p, g]) >= 10]
            a[p, g + 8] = far[np.random.randint(len(far))]
    return np.exp2(a.ravel()).repeat(32)


def f64(x):
    return np.asarray(x).astype(np.float64)


def striped8(idx):
    return np.asarray(idx).reshape(8, -1, 16).transpose(0, 2, 1).reshape(128, -1).astype(np.uint16)


def unstriped8(offs):
    return offs.reshape(8, 16, -1).transpose(0, 2, 1).reshape(8, -1).astype(np.int64)


def pick8(x, idx, run):
    r = np.arange(len(x))
    return x[r[:, None], idx[r % (8 * run) // run]]


E2M1 = np.array([0.0, 0.5, 1.0, 1.5, 2.0, 3.0, 4.0, 6.0, -0.0, -0.5, -1.0, -1.5, -2.0, -3.0, -4.0, -6.0])


def pack_weight(w, fmt):
    k, n = w.shape
    w = f64(np.asarray(w, np.float32).astype(ml_dtypes.bfloat16)).reshape(k // 32, 32, n)
    amax = np.abs(w).max(1)
    if fmt == "e4m3":
        byte = np.frexp(amax)[1] - 1 + 127 - 7
    else:
        mant, ex = np.frexp(amax / 6.0)
        byte = np.where(mant > 0.5, ex, ex - 1) + 127
    byte = np.clip(np.where(amax > 0, byte, 1), 1, 254)
    scaled = (w * np.exp2(127.0 - byte)[:, None, :]).reshape(k, n).astype(np.float32)
    by_word = np.ascontiguousarray(scaled.reshape(k // 512, 128, 4, n).transpose(0, 1, 3, 2))
    if fmt == "e4m3":
        words = by_word.astype(ml_dtypes.float8_e4m3fn).view(np.uint8)
    else:
        c = by_word.astype(ml_dtypes.float4_e2m1fn).view(np.uint8) & 0xF
        words = (c[..., 0::2] | (c[..., 1::2] << 4)).reshape(k // 512, 128, 2 * n)
    return np.ascontiguousarray(words), np.ascontiguousarray(byte.astype(np.uint8).reshape(k // 512, 16, n))


def unpack_weight(words, scales, fmt):
    g, _, n = scales.shape
    words = np.ascontiguousarray(words).reshape(g, 128, n, -1)
    if fmt == "e4m3":
        vals = words.view(ml_dtypes.float8_e4m3fn).astype(np.float64)
    else:
        nib = np.empty((g, 128, n, 4), np.uint8)
        nib[..., 0::2] = words & 0xF
        nib[..., 1::2] = words >> 4
        vals = E2M1[nib]
    vals = vals * np.repeat(np.exp2(scales.astype(np.float64) - 127.0), 8, axis=1)[..., None]
    return vals.transpose(0, 1, 3, 2).reshape(g * 512, n)


D, T, U, X, I, Q = 512, 1024, 1024, 1024, 512, 128


def setup_inputs():
    n = np.random.standard_normal
    idx = np.stack([np.random.permutation(U)[:I] for _ in range(8)])
    idx2 = np.stack([np.random.permutation(U)[:I] for _ in range(8)])
    idx3 = np.stack([np.random.permutation(U)[:I] for _ in range(8)])
    idx4 = np.stack([np.random.permutation(T)[:I] for _ in range(8)])
    idx5 = np.stack([np.random.permutation(X)[:I] for _ in range(8)])
    idx6 = np.stack([np.random.permutation(X)[:I] for _ in range(8)])
    fd = mx_kscale(D)
    cachep = pack_weight(n((D, T)) / fd[:, None], "e2m1")
    draftp = pack_weight(n((D, U)) / fd[:, None], "e4m3")
    archp = pack_weight(n((D, X)) / fd[:, None], "e2m1")
    return {
        "query": (n((D, Q)) * 1.0 / np.sqrt(D) * fd[:, None]).astype(np.float32),
        "cache_words": cachep[0],
        "cache_scales": cachep[1],
        "draft_words": draftp[0],
        "draft_scales": draftp[1],
        "arch_words": archp[0],
        "arch_scales": archp[1],
        "offs": striped8(idx),
        "offs2": striped8(idx2),
        "offs3": striped8(idx3),
        "offs4": striped8(idx4),
        "offs5": striped8(idx5),
        "offs6": striped8(idx6),
    }


def reference(query, cache_words, cache_scales, draft_words, draft_scales, arch_words, arch_scales, offs, offs2, offs3, offs4, offs5, offs6):
    idx = unstriped8(offs)
    idx2 = unstriped8(offs2)
    idx3 = unstriped8(offs3)
    idx4 = unstriped8(offs4)
    idx5 = unstriped8(offs5)
    idx6 = unstriped8(offs6)
    cacheu = unpack_weight(cache_words, cache_scales, "e2m1")
    draftu = unpack_weight(draft_words, draft_scales, "e4m3")
    archu = unpack_weight(arch_words, arch_scales, "e2m1")
    queryq = mxq(f64(query), 0, "e4m3")
    a = queryq.T @ cacheu
    b = queryq.T @ draftu
    c0 = queryq.T @ archu
    nb = np.zeros((Q, U))
    nb[np.arange(Q)[:, None], idx2[np.arange(Q) % 128 // 16]] = pick8(b, idx, 16)
    w = pick8(nb, idx3, 16) + pick8(a, idx4, 16)
    f1 = np.zeros((Q, X))
    f1[np.arange(Q)[:, None], idx5[np.arange(Q) % 128 // 16]] = w
    cc = np.maximum(c0, f1)
    y = pick8(cc, idx6, 16) - w
    return y

@@ -1,0 +1,156 @@
+from contextlib import ExitStack
+
+import concourse.mybir as mybir
+
+F32 = mybir.dt.float32
+BF16 = mybir.dt.bfloat16
+I32 = mybir.dt.int32
+U32 = mybir.dt.uint32
+U16 = mybir.dt.uint16
+U8 = mybir.dt.uint8
+FP8X4 = mybir.dt.float8_e4m3fn_x4
+FP4X4 = mybir.dt.float4_e2m1fn_x4
+COPY = mybir.ActivationFunctionType.Copy
+ADD = mybir.AluOpType.add
+SUB = mybir.AluOpType.subtract
+MAX = mybir.AluOpType.max
+
+P = 128
+PACK = 4
+D = 512
+Q = 128
+TOKENS = 1024
+SLOTS = 512
+GROUP = 16
+HALF = SLOTS // 2
+BANK = 512
+DRAFT_N = 256
+
+FLOPS = 2 * D * Q * 3 * TOKENS
+
+
+def load_scales(engine, plane, scales):
+    rows = scales[0].bitcast(I32)
+    for quad in range(4):
+        engine.dma_start(plane[32 * quad : 32 * quad + 4, :].bitcast(I32), rows[4 * quad : 4 * quad + 4, :])
+
+
+def entries(offsets, half):
+    cols = HALF // GROUP
+    return offsets[:, half * cols : (half + 1) * cols]
+
+
+def tile_attend_beamstep_three_kernel(
+    tc, query, cache_words, cache_scales, draft_words, draft_scales, arch_words, arch_scales,
+    offs, offs2, offs3, offs4, offs5, offs6, out,
+):
+    nc = tc.nc
+    with ExitStack() as ctx:
+        sb = ctx.enter_context(tc.tile_pool(name="sb", bufs=1))
+        ps = ctx.enter_context(tc.psum_pool(name="ps", bufs=1))
+
+        def slot_cols(half):
+            return slice(half * HALF, (half + 1) * HALF)
+
+        def load_list(name, source):
+            tile = sb.tile([P, SLOTS // GROUP], U16, name=name)
+            nc.sync.dma_start(tile[:], source)
+            return tile
+
+        draft_plane = sb.tile([P, TOKENS], U8, name="draft_plane", align_bytes=64)
+        cache_plane = sb.tile([P, TOKENS], U8, name="cache_plane", align_bytes=64)
+        arch_plane = sb.tile([P, TOKENS], U8, name="arch_plane", align_bytes=64)
+        nb = sb.tile([P, TOKENS], F32, name="nb")
+        f1 = sb.tile([P, TOKENS], F32, name="f1")
+        nc.vector.memset(draft_plane[:].bitcast(I32), 0)
+        nc.vector.memset(cache_plane[:].bitcast(I32), 0)
+        nc.vector.memset(arch_plane[:].bitcast(I32), 0)
+        nc.vector.memset(nb[:], 0.0)
+        nc.vector.memset(f1[:], 0.0)
+
+        q_raw = sb.tile([P, PACK, Q], F32, name="q_raw")
+        nc.sync.dma_start(q_raw[:], query.rearrange("(p j) q -> p j q", j=PACK))
+        load_scales(nc.scalar, draft_plane, draft_scales)
+        draft_src = draft_words[0].rearrange("p n t -> p (n t)").bitcast(I32)
+        draft_halves = []
+        for h in range(TOKENS // BANK):
+            words = sb.tile([P, BANK], U32, name="draft_words%d" % h, align_bytes=64)
+            nc.sync.dma_start(words[:].bitcast(I32), draft_src[:, h * BANK : (h + 1) * BANK])
+            draft_halves.append(words)
+        idx = load_list("idx", offs)
+        idx2 = load_list("idx2", offs2)
+        cache_sb = sb.tile([P, 2 * TOKENS], U8, name="cache_sb", align_bytes=64)
+        nc.sync.dma_start(cache_sb[:].bitcast(I32), cache_words[0].bitcast(I32))
+        load_scales(nc.sync, cache_plane, cache_scales)
+        idx4 = load_list("idx4", offs4)
+        idx3 = load_list("idx3", offs3)
+        idx5 = load_list("idx5", offs5)
+        arch_sb = sb.tile([P, 2 * TOKENS], U8, name="arch_sb", align_bytes=64)
+        nc.sync.dma_start(arch_sb[:].bitcast(I32), arch_words[0].bitcast(I32))
+        load_scales(nc.sync, arch_plane, arch_scales)
+        idx6 = load_list("idx6", offs6)
+
+        q_bf = sb.tile([P, Q, PACK], BF16, name="q_bf", align_bytes=64)
+        nc.vector.tensor_copy(q_bf[:], q_raw[:].rearrange("p j q -> p q j"))
+        q_codes = sb.tile([P, Q], U32, name="q_codes", align_bytes=64)
+        q_plane = sb.tile([P, Q], U8, name="q_plane", align_bytes=64)
+        nc.vector.quantize_mx(
+            out=q_codes[:].bitcast(FP8X4), scales=q_plane[:], in_=q_bf[:].rearrange("p q j -> p (q j)")
+        )
+
+        def score(name, codes, plane, width):
+            bank = ps.tile([Q, width], F32, name=name)
+            nc.tensor.matmul_mx(
+                out=bank[:], lhsT=q_codes[:].bitcast(FP8X4), lhsT_scale=q_plane[:],
+                rhs=codes, rhs_scale=plane, start=True, stop=True,
+            )
+            return bank
+
+        b = sb.tile([Q, TOKENS], F32, name="b")
+        for piece in range(TOKENS // DRAFT_N):
+            first = piece * DRAFT_N
+            words = draft_halves[first // BANK][:, first % BANK : first % BANK + DRAFT_N]
+            cols = slice(first, first + DRAFT_N)
+            bank = score("b%d" % piece, words.bitcast(FP8X4), draft_plane[:, cols], DRAFT_N)
+            if piece % 2 == 0:
+                nc.vector.tensor_copy(b[:, cols], bank[:])
+            else:
+                nc.scalar.activation(b[:, cols], bank[:], COPY)
+
+        def score_fp4(name, words, plane):
+            return [
+                score("%s%d" % (name, h), words[:, 2 * h * BANK : 2 * (h + 1) * BANK].bitcast(FP4X4),
+                      plane[:, h * BANK : (h + 1) * BANK], BANK)
+                for h in range(TOKENS // BANK)
+            ]
+
+        a_banks = score_fp4("a", cache_sb, cache_plane)
+        c0_banks = score_fp4("c", arch_sb, arch_plane)
+
+        picked = [sb.tile([Q, HALF], F32, name="picked%d" % h) for h in range(2)]
+        for h in range(2):
+            nc.vector.tensor_copy(picked[h][:], b[:].indirect(entries(idx, h)))
+        for h in range(2):
+            nc.scalar.activation(nb[:].indirect(entries(idx2, h)), picked[h][:], COPY)
+
+        a = sb.tile([Q, TOKENS], F32, name="a")
+        for h in range(2):
+            nc.vector.tensor_copy(a[:, h * BANK : (h + 1) * BANK], a_banks[h][:])
+        cached = [sb.tile([Q, HALF], F32, name="cached%d" % h) for h in range(2)]
+        w = [sb.tile([Q, HALF], F32, name="w%d" % h) for h in range(2)]
+        for h in range(2):
+            nc.vector.tensor_copy(cached[h][:], a[:].indirect(entries(idx4, h)))
+        for h in range(2):
+            nc.vector.tensor_tensor(w[h][:], nb[:].indirect(entries(idx3, h)), cached[h][:], ADD)
+        for h in range(2):
+            nc.scalar.activation(f1[:].indirect(entries(idx5, h)), w[h][:], COPY)
+
+        cc = sb.tile([Q, TOKENS], F32, name="cc")
+        for h in range(2):
+            cols = slice(h * BANK, (h + 1) * BANK)
+            nc.vector.tensor_tensor(cc[:, cols], c0_banks[h][:], f1[:, cols], MAX)
+
+        for h in range(2):
+            result = sb.tile([Q, HALF], F32, name="result%d" % h)
+            nc.vector.tensor_tensor(result[:], cc[:].indirect(entries(idx6, h)), w[h][:], SUB)
+            nc.sync.dma_start(out[:, slot_cols(h)], result[:])

@@ -25,14 +25,16 @@ GROUP = 16
 HALF = SLOTS // 2
 BANK = 512
 DRAFT_N = 256
+DRAFT_WIDTHS = (256, 256, 256, 128, 128)
+VECTOR_ROWS = 80
 
 FLOPS = 2 * D * Q * 3 * TOKENS
 
 
-def load_scales(engine, plane, scales):
+def load_scales(engines, plane, scales):
     rows = scales[0].bitcast(I32)
     for quad in range(4):
-        engine.dma_start(plane[32 * quad : 32 * quad + 4, :].bitcast(I32), rows[4 * quad : 4 * quad + 4, :])
+        engines[quad % len(engines)].dma_start(plane[32 * quad : 32 * quad + 4, :].bitcast(I32), rows[4 * quad : 4 * quad + 4, :])
 
 
 def entries(offsets, half):
@@ -57,49 +59,59 @@ def tile_attend_beamstep_three_kernel(
             nc.sync.dma_start(tile[:], source)
             return tile
 
-        draft_plane = sb.tile([P, TOKENS], U8, name="draft_plane", align_bytes=64)
+        draft_plane = sb.tile([P, DRAFT_N], U8, name="draft_plane", align_bytes=64)
         cache_plane = sb.tile([P, TOKENS], U8, name="cache_plane", align_bytes=64)
         arch_plane = sb.tile([P, TOKENS], U8, name="arch_plane", align_bytes=64)
         nb = sb.tile([P, TOKENS], F32, name="nb")
-        f1 = sb.tile([P, TOKENS], F32, name="f1")
         nc.vector.memset(draft_plane[:].bitcast(I32), 0)
         nc.vector.memset(cache_plane[:].bitcast(I32), 0)
         nc.vector.memset(arch_plane[:].bitcast(I32), 0)
         nc.vector.memset(nb[:], 0.0)
-        nc.vector.memset(f1[:], 0.0)
 
         q_raw = sb.tile([P, PACK, Q], F32, name="q_raw")
         nc.sync.dma_start(q_raw[:], query.rearrange("(p j) q -> p j q", j=PACK))
-        load_scales(nc.scalar, draft_plane, draft_scales)
-        draft_src = draft_words[0].rearrange("p n t -> p (n t)").bitcast(I32)
-        draft_halves = []
-        for h in range(TOKENS // BANK):
-            words = sb.tile([P, BANK], U32, name="draft_words%d" % h, align_bytes=64)
-            nc.sync.dma_start(words[:].bitcast(I32), draft_src[:, h * BANK : (h + 1) * BANK])
-            draft_halves.append(words)
         idx = load_list("idx", offs)
+        draft_src = draft_words[0].rearrange("p n t -> p (n t)").bitcast(I32)
+        draft_halves = [sb.tile([P, BANK], U32, name="draft_words%d" % h, align_bytes=64) for h in range(2)]
+        nc.sync.dma_start(draft_halves[0][:].bitcast(I32), draft_src[:, :BANK])
+        draft_rows = draft_scales[0].bitcast(I32).rearrange("r (j n) -> j r n", j=4)
+        for quad in range(4):
+            nc.sync.dma_start(
+                draft_plane[32 * quad : 32 * quad + 16, :].bitcast(I32), draft_rows[:, 4 * quad : 4 * quad + 4, :]
+            )
+        nc.sync.dma_start(draft_halves[1][:].bitcast(I32), draft_src[:, BANK:])
         idx2 = load_list("idx2", offs2)
         cache_sb = sb.tile([P, 2 * TOKENS], U8, name="cache_sb", align_bytes=64)
         nc.sync.dma_start(cache_sb[:].bitcast(I32), cache_words[0].bitcast(I32))
-        load_scales(nc.sync, cache_plane, cache_scales)
+        load_scales([nc.sync], cache_plane, cache_scales)
         idx4 = load_list("idx4", offs4)
         idx3 = load_list("idx3", offs3)
         idx5 = load_list("idx5", offs5)
         arch_sb = sb.tile([P, 2 * TOKENS], U8, name="arch_sb", align_bytes=64)
         nc.sync.dma_start(arch_sb[:].bitcast(I32), arch_words[0].bitcast(I32))
-        load_scales(nc.sync, arch_plane, arch_scales)
+        load_scales([nc.sync], arch_plane, arch_scales)
         idx6 = load_list("idx6", offs6)
 
-        q_bf = sb.tile([P, Q, PACK], BF16, name="q_bf", align_bytes=64)
-        nc.vector.tensor_copy(q_bf[:], q_raw[:].rearrange("p j q -> p q j"))
+        q_bf = sb.tile([P, Q, PACK], BF16, name="q_bf", tag="q_bf_then_f1", align_bytes=64)
+        def woven(first, last):
+            return (
+                q_bf[:, first:last, :].rearrange("p (c i) j -> p c j i", i=4),
+                q_raw[:, :, first:last].rearrange("p j (c i) -> p c j i", i=4),
+            )
+
+        nc.vector.tensor_copy(*woven(0, VECTOR_ROWS))
+        nc.scalar.activation(*woven(VECTOR_ROWS, Q), COPY)
         q_codes = sb.tile([P, Q], U32, name="q_codes", align_bytes=64)
         q_plane = sb.tile([P, Q], U8, name="q_plane", align_bytes=64)
         nc.vector.quantize_mx(
             out=q_codes[:].bitcast(FP8X4), scales=q_plane[:], in_=q_bf[:].rearrange("p q j -> p (q j)")
         )
 
-        def score(name, codes, plane, width):
-            bank = ps.tile([Q, width], F32, name=name)
+        f1 = sb.tile([P, TOKENS], F32, name="f1", tag="q_bf_then_f1", align_bytes=64)
+        nc.gpsimd.memset(f1[:], 0.0)
+
+        def score(name, tag, codes, plane, width):
+            bank = ps.tile([Q, width], F32, name=name, tag=tag)
             nc.tensor.matmul_mx(
                 out=bank[:], lhsT=q_codes[:].bitcast(FP8X4), lhsT_scale=q_plane[:],
                 rhs=codes, rhs_scale=plane, start=True, stop=True,
@@ -107,31 +119,32 @@ def tile_attend_beamstep_three_kernel(
             return bank
 
         b = sb.tile([Q, TOKENS], F32, name="b")
-        for piece in range(TOKENS // DRAFT_N):
-            first = piece * DRAFT_N
-            words = draft_halves[first // BANK][:, first % BANK : first % BANK + DRAFT_N]
-            cols = slice(first, first + DRAFT_N)
-            bank = score("b%d" % piece, words.bitcast(FP8X4), draft_plane[:, cols], DRAFT_N)
+        first = 0
+        for piece, width in enumerate(DRAFT_WIDTHS):
+            words = draft_halves[first // BANK][:, first % BANK : first % BANK + width]
+            cols = slice(first, first + width)
+            plane = draft_plane[4 * (first // DRAFT_N) :, first % DRAFT_N : first % DRAFT_N + width]
+            bank = score("b%d" % piece, "bank%d" % piece, words.bitcast(FP8X4), plane, width)
             if piece % 2 == 0:
                 nc.vector.tensor_copy(b[:, cols], bank[:])
             else:
                 nc.scalar.activation(b[:, cols], bank[:], COPY)
+            first = first + width
 
-        def score_fp4(name, words, plane):
+        def score_fp4(name, tags, words, plane):
             return [
-                score("%s%d" % (name, h), words[:, 2 * h * BANK : 2 * (h + 1) * BANK].bitcast(FP4X4),
+                score("%s%d" % (name, h), tags[h], words[:, 2 * h * BANK : 2 * (h + 1) * BANK].bitcast(FP4X4),
                       plane[:, h * BANK : (h + 1) * BANK], BANK)
                 for h in range(TOKENS // BANK)
             ]
 
-        a_banks = score_fp4("a", cache_sb, cache_plane)
-        c0_banks = score_fp4("c", arch_sb, arch_plane)
+        a_banks = score_fp4("a", ["bank5", "bank6"], cache_sb, cache_plane)
+        c0_banks = score_fp4("c", ["bank7", "bank0"], arch_sb, arch_plane)
 
-        picked = [sb.tile([Q, HALF], F32, name="picked%d" % h) for h in range(2)]
-        for h in range(2):
-            nc.vector.tensor_copy(picked[h][:], b[:].indirect(entries(idx, h)))
-        for h in range(2):
-            nc.scalar.activation(nb[:].indirect(entries(idx2, h)), picked[h][:], COPY)
+        picked = sb.tile([Q, SLOTS], F32, name="picked")
+        nc.vector.tensor_copy(picked[:, slot_cols(0)], b[:].indirect(entries(idx, 0)))
+        nc.scalar.activation(picked[:, slot_cols(1)], b[:].indirect(entries(idx, 1)), COPY)
+        nc.scalar.activation(nb[:].indirect(idx2[:]), picked[:], COPY)
 
         a = sb.tile([Q, TOKENS], F32, name="a")
         for h in range(2):
@@ -140,7 +153,6 @@ def tile_attend_beamstep_three_kernel(
         w = [sb.tile([Q, HALF], F32, name="w%d" % h) for h in range(2)]
         for h in range(2):
             nc.vector.tensor_copy(cached[h][:], a[:].indirect(entries(idx4, h)))
-        for h in range(2):
             nc.vector.tensor_tensor(w[h][:], nb[:].indirect(entries(idx3, h)), cached[h][:], ADD)
         for h in range(2):
             nc.scalar.activation(f1[:].indirect(entries(idx5, h)), w[h][:], COPY)

@@ -162,7 +162,13 @@ def tile_attend_beamstep_three_kernel(
             cols = slice(h * BANK, (h + 1) * BANK)
             nc.vector.tensor_tensor(cc[:, cols], c0_banks[h][:], f1[:, cols], MAX)
 
-        for h in range(2):
-            result = sb.tile([Q, HALF], F32, name="result%d" % h)
-            nc.vector.tensor_tensor(result[:], cc[:].indirect(entries(idx6, h)), w[h][:], SUB)
-            nc.sync.dma_start(out[:, slot_cols(h)], result[:])
+        first_result = sb.tile([Q, HALF], F32, name="first_result")
+        best = sb.tile([Q, HALF], F32, name="best")
+        nc.vector.tensor_tensor(first_result[:], cc[:].indirect(entries(idx6, 0)), w[0][:], SUB)
+        nc.scalar.activation(best[:], cc[:].indirect(entries(idx6, 1)), COPY)
+        nc.sync.dma_start(out[:, slot_cols(0)], first_result[:])
+        for part in range(2):
+            cols = slice(part * HALF // 2, (part + 1) * HALF // 2)
+            result = sb.tile([Q, HALF // 2], F32, name="result%d" % part)
+            nc.vector.tensor_tensor(result[:], best[:, cols], w[1][:, cols], SUB)
+            nc.sync.dma_start(out[:, HALF + cols.start : HALF + cols.stop], result[:])

from contextlib import ExitStack

import concourse.mybir as mybir

F32 = mybir.dt.float32
BF16 = mybir.dt.bfloat16
I32 = mybir.dt.int32
U32 = mybir.dt.uint32
U16 = mybir.dt.uint16
U8 = mybir.dt.uint8
FP8X4 = mybir.dt.float8_e4m3fn_x4
FP4X4 = mybir.dt.float4_e2m1fn_x4
COPY = mybir.ActivationFunctionType.Copy
ADD = mybir.AluOpType.add
SUB = mybir.AluOpType.subtract
MAX = mybir.AluOpType.max

P = 128
PACK = 4
D = 512
Q = 128
TOKENS = 1024
SLOTS = 512
GROUP = 16
HALF = SLOTS // 2
BANK = 512
DRAFT_N = 256
DRAFT_WIDTHS = (256, 256, 256, 128, 128)
VECTOR_ROWS = 80

FLOPS = 2 * D * Q * 3 * TOKENS


def load_scales(engines, plane, scales):
    rows = scales[0].bitcast(I32)
    for quad in range(4):
        engines[quad % len(engines)].dma_start(plane[32 * quad : 32 * quad + 4, :].bitcast(I32), rows[4 * quad : 4 * quad + 4, :])


def entries(offsets, half):
    cols = HALF // GROUP
    return offsets[:, half * cols : (half + 1) * cols]


def tile_attend_beamstep_three_kernel(
    tc, query, cache_words, cache_scales, draft_words, draft_scales, arch_words, arch_scales,
    offs, offs2, offs3, offs4, offs5, offs6, out,
):
    nc = tc.nc
    with ExitStack() as ctx:
        sb = ctx.enter_context(tc.tile_pool(name="sb", bufs=1))
        ps = ctx.enter_context(tc.psum_pool(name="ps", bufs=1))

        def slot_cols(half):
            return slice(half * HALF, (half + 1) * HALF)

        def load_list(name, source):
            tile = sb.tile([P, SLOTS // GROUP], U16, name=name)
            nc.sync.dma_start(tile[:], source)
            return tile

        draft_plane = sb.tile([P, DRAFT_N], U8, name="draft_plane", align_bytes=64)
        cache_plane = sb.tile([P, TOKENS], U8, name="cache_plane", align_bytes=64)
        arch_plane = sb.tile([P, TOKENS], U8, name="arch_plane", align_bytes=64)
        nb = sb.tile([P, TOKENS], F32, name="nb")
        nc.vector.memset(draft_plane[:].bitcast(I32), 0)
        nc.vector.memset(cache_plane[:].bitcast(I32), 0)
        nc.vector.memset(arch_plane[:].bitcast(I32), 0)
        nc.vector.memset(nb[:], 0.0)

        q_raw = sb.tile([P, PACK, Q], F32, name="q_raw")
        nc.sync.dma_start(q_raw[:], query.rearrange("(p j) q -> p j q", j=PACK))
        idx = load_list("idx", offs)
        draft_src = draft_words[0].rearrange("p n t -> p (n t)").bitcast(I32)
        draft_halves = [sb.tile([P, BANK], U32, name="draft_words%d" % h, align_bytes=64) for h in range(2)]
        nc.sync.dma_start(draft_halves[0][:].bitcast(I32), draft_src[:, :BANK])
        draft_rows = draft_scales[0].bitcast(I32).rearrange("r (j n) -> j r n", j=4)
        for quad in range(4):
            nc.sync.dma_start(
                draft_plane[32 * quad : 32 * quad + 16, :].bitcast(I32), draft_rows[:, 4 * quad : 4 * quad + 4, :]
            )
        nc.sync.dma_start(draft_halves[1][:].bitcast(I32), draft_src[:, BANK:])
        idx2 = load_list("idx2", offs2)
        cache_sb = sb.tile([P, 2 * TOKENS], U8, name="cache_sb", align_bytes=64)
        nc.sync.dma_start(cache_sb[:].bitcast(I32), cache_words[0].bitcast(I32))
        load_scales([nc.sync], cache_plane, cache_scales)
        idx4 = load_list("idx4", offs4)
        idx3 = load_list("idx3", offs3)
        idx5 = load_list("idx5", offs5)
        arch_sb = sb.tile([P, 2 * TOKENS], U8, name="arch_sb", align_bytes=64)
        nc.sync.dma_start(arch_sb[:].bitcast(I32), arch_words[0].bitcast(I32))
        load_scales([nc.sync], arch_plane, arch_scales)
        idx6 = load_list("idx6", offs6)

        q_bf = sb.tile([P, Q, PACK], BF16, name="q_bf", tag="q_bf_then_f1", align_bytes=64)
        def woven(first, last):
            return (
                q_bf[:, first:last, :].rearrange("p (c i) j -> p c j i", i=4),
                q_raw[:, :, first:last].rearrange("p j (c i) -> p c j i", i=4),
            )

        nc.vector.tensor_copy(*woven(0, VECTOR_ROWS))
        nc.scalar.activation(*woven(VECTOR_ROWS, Q), COPY)
        q_codes = sb.tile([P, Q], U32, name="q_codes", align_bytes=64)
        q_plane = sb.tile([P, Q], U8, name="q_plane", align_bytes=64)
        nc.vector.quantize_mx(
            out=q_codes[:].bitcast(FP8X4), scales=q_plane[:], in_=q_bf[:].rearrange("p q j -> p (q j)")
        )

        f1 = sb.tile([P, TOKENS], F32, name="f1", tag="q_bf_then_f1", align_bytes=64)
        nc.gpsimd.memset(f1[:], 0.0)

        def score(name, tag, codes, plane, width):
            bank = ps.tile([Q, width], F32, name=name, tag=tag)
            nc.tensor.matmul_mx(
                out=bank[:], lhsT=q_codes[:].bitcast(FP8X4), lhsT_scale=q_plane[:],
                rhs=codes, rhs_scale=plane, start=True, stop=True,
            )
            return bank

        b = sb.tile([Q, TOKENS], F32, name="b")
        first = 0
        for piece, width in enumerate(DRAFT_WIDTHS):
            words = draft_halves[first // BANK][:, first % BANK : first % BANK + width]
            cols = slice(first, first + width)
            plane = draft_plane[4 * (first // DRAFT_N) :, first % DRAFT_N : first % DRAFT_N + width]
            bank = score("b%d" % piece, "bank%d" % piece, words.bitcast(FP8X4), plane, width)
            if piece % 2 == 0:
                nc.vector.tensor_copy(b[:, cols], bank[:])
            else:
                nc.scalar.activation(b[:, cols], bank[:], COPY)
            first = first + width

        def score_fp4(name, tags, words, plane):
            return [
                score("%s%d" % (name, h), tags[h], words[:, 2 * h * BANK : 2 * (h + 1) * BANK].bitcast(FP4X4),
                      plane[:, h * BANK : (h + 1) * BANK], BANK)
                for h in range(TOKENS // BANK)
            ]

        a_banks = score_fp4("a", ["bank5", "bank6"], cache_sb, cache_plane)
        c0_banks = score_fp4("c", ["bank7", "bank0"], arch_sb, arch_plane)

        picked = sb.tile([Q, SLOTS], F32, name="picked")
        nc.vector.tensor_copy(picked[:, slot_cols(0)], b[:].indirect(entries(idx, 0)))
        nc.scalar.activation(picked[:, slot_cols(1)], b[:].indirect(entries(idx, 1)), COPY)
        nc.scalar.activation(nb[:].indirect(idx2[:]), picked[:], COPY)

        a = sb.tile([Q, TOKENS], F32, name="a")
        for h in range(2):
            nc.vector.tensor_copy(a[:, h * BANK : (h + 1) * BANK], a_banks[h][:])
        cached = [sb.tile([Q, HALF], F32, name="cached%d" % h) for h in range(2)]
        w = [sb.tile([Q, HALF], F32, name="w%d" % h) for h in range(2)]
        for h in range(2):
            nc.vector.tensor_copy(cached[h][:], a[:].indirect(entries(idx4, h)))
            nc.vector.tensor_tensor(w[h][:], nb[:].indirect(entries(idx3, h)), cached[h][:], ADD)
        for h in range(2):
            nc.scalar.activation(f1[:].indirect(entries(idx5, h)), w[h][:], COPY)

        cc = sb.tile([Q, TOKENS], F32, name="cc")
        for h in range(2):
            cols = slice(h * BANK, (h + 1) * BANK)
            nc.vector.tensor_tensor(cc[:, cols], c0_banks[h][:], f1[:, cols], MAX)

        first_result = sb.tile([Q, HALF], F32, name="first_result")
        best = sb.tile([Q, HALF], F32, name="best")
        nc.vector.tensor_tensor(first_result[:], cc[:].indirect(entries(idx6, 0)), w[0][:], SUB)
        nc.scalar.activation(best[:], cc[:].indirect(entries(idx6, 1)), COPY)
        nc.sync.dma_start(out[:, slot_cols(0)], first_result[:])
        for part in range(2):
            cols = slice(part * HALF // 2, (part + 1) * HALF // 2)
            result = sb.tile([Q, HALF // 2], F32, name="result%d" % part)
            nc.vector.tensor_tensor(result[:], best[:, cols], w[1][:, cols], SUB)
            nc.sync.dma_start(out[:, HALF + cols.start : HALF + cols.stop], result[:])
